import numpy as np
import ml_dtypes


def mxq(x, axis, fmt="e4m3"):
    dtype, down = {"e4m3": (ml_dtypes.float8_e4m3fn, 7), "e5m2": (ml_dtypes.float8_e5m2, 14)}[fmt]
    v = np.moveaxis(np.asarray(x, np.float32).astype(ml_dtypes.bfloat16).astype(np.float64), axis, -1)
    blocks = v.reshape(v.shape[:-1] + (-1, 32))
    amax = np.abs(blocks).max(-1, keepdims=True)
    byte = np.maximum(np.where(amax > 0, np.frexp(amax)[1] - 1 + 127, 0) - down, 1)
    scale = np.exp2(byte - 127.0)
    codes = (blocks / scale).astype(np.float32).astype(dtype).astype(np.float64)
    return np.moveaxis((codes * scale).reshape(v.shape), -1, axis)


WIDE = False


def mx_kscale(k):
    if not WIDE:
        return np.ones(k)
    levels = np.array([10, -10, 5, -5, 0])
    if k % 512:
        return np.exp2(np.random.permutation(np.resize(levels, k // 32))).repeat(32)
    a = np.empty((k // 512, 16))
    for p in range(k // 512):
        a[p, :8] = np.random.permutation(np.resize(levels, 8))
        for g in range(8):
            far = levels[np.abs(levels - a[p, g]) >= 10]
            a[p, g + 8] = far[np.random.randint(len(far))]
    return np.exp2(a.ravel()).repeat(32)


def f64(x):
    return np.asarray(x).astype(np.float64)


def striped8(idx):
    return np.concatenate([v.reshape(-1, 16).T for v in idx]).astype(np.uint16)


def unstriped8(offs):
    return np.stack([offs[16 * g:16 * g + 16].T.reshape(-1) for g in range(8)]).astype(np.int64)


E2M1 = np.array([0.0, 0.5, 1.0, 1.5, 2.0, 3.0, 4.0, 6.0, -0.0, -0.5, -1.0, -1.5, -2.0, -3.0, -4.0, -6.0])


def pack_weight(w, fmt):
    k, n = w.shape
    w = f64(np.asarray(w, np.float32).astype(ml_dtypes.bfloat16)).reshape(k // 32, 32, n)
    amax = np.abs(w).max(1)
    if fmt == "e4m3":
        byte = np.frexp(amax)[1] - 1 + 127 - 7
    else:
        mant, ex = np.frexp(amax / 6.0)
        byte = np.where(mant > 0.5, ex, ex - 1) + 127
    byte = np.clip(np.where(amax > 0, byte, 1), 1, 254)
    scaled = (w * np.exp2(127.0 - byte)[:, None, :]).reshape(k, n).astype(np.float32)
    by_word = np.ascontiguousarray(scaled.reshape(k // 512, 128, 4, n).transpose(0, 1, 3, 2))
    if fmt == "e4m3":
        words = by_word.astype(ml_dtypes.float8_e4m3fn).view(np.uint8)
    else:
        c = by_word.astype(ml_dtypes.float4_e2m1fn).view(np.uint8) & 0xF
        words = (c[..., 0::2] | (c[..., 1::2] << 4)).reshape(k // 512, 128, 2 * n)
    return np.ascontiguousarray(words), np.ascontiguousarray(byte.astype(np.uint8).reshape(k // 512, 16, n))


def unpack_weight(words, scales, fmt):
    g, _, n = scales.shape
    words = np.ascontiguousarray(words).reshape(g, 128, n, -1)
    if fmt == "e4m3":
        vals = words.view(ml_dtypes.float8_e4m3fn).astype(np.float64)
    else:
        nib = np.empty((g, 128, n, 4), np.uint8)
        nib[..., 0::2] = words & 0xF
        nib[..., 1::2] = words >> 4
        vals = E2M1[nib]
    vals = vals * np.repeat(np.exp2(scales.astype(np.float64) - 127.0), 8, axis=1)[..., None]
    return vals.transpose(0, 1, 3, 2).reshape(g * 512, n)


K, M, T, S = 512, 256, 1024, 512


def setup_inputs():
    n = np.random.standard_normal
    s = mx_kscale(K)[:, None]
    w = n((K, M)) / np.sqrt(K) / s
    w4 = pack_weight(w, "e2m1")
    rest = w - unpack_weight(*w4, "e2m1")
    p_r8 = pack_weight(rest, "e4m3")
    return {
        "xT": (n((K, T)) * s).astype(np.float32),
        "w4_words": w4[0],
        "w4_scales": w4[1],
        "r8_words": p_r8[0],
        "r8_scales": p_r8[1],
        "wgt": np.repeat(np.random.uniform(0.5, 2.0, (8, S)), 16, axis=0).astype(np.float32),
        "b": (0.3 * n(256)).astype(np.float32),
        "wgo": np.repeat(np.random.uniform(0.5, 2.0, (8, S)), 16, axis=0).astype(np.float32),
        "offs": striped8(np.stack([np.random.permutation(T)[:S] for _ in range(8)])),
        "offs2": striped8(np.stack([np.random.permutation(T)[:S] for _ in range(8)])),
    }


def reference(xT, w4_words, w4_scales, r8_words, r8_scales, wgt, b, wgo, offs, offs2):
    idx = unstriped8(offs)
    group = np.arange(K) % 512 // 64
    xg = f64(wgt)[np.arange(K) // 4 % 128] * f64(xT)[np.arange(K)[:, None], idx[group]]
    xT_ = mxq(xg, 0, "e4m3")
    w4_ = unpack_weight(w4_words, w4_scales, "e2m1")
    r8_ = unpack_weight(r8_words, r8_scales, "e4m3")
    y = w4_.T @ xT_ + r8_.T @ xT_
    place = unstriped8(offs2)[np.arange(M) % 128 // 16]
    out = np.zeros((M, T))
    out[np.arange(M)[:, None], place] = f64(wgo)[np.arange(M) % 128] * (y + f64(b)[:, None])
    return out

@@ -1,0 +1,157 @@
+from contextlib import ExitStack
+
+import concourse.mybir as mybir
+
+K, M, T, S = 512, 256, 1024, 512
+
+F32 = mybir.dt.float32
+BF16 = mybir.dt.bfloat16
+I32 = mybir.dt.int32
+U32 = mybir.dt.uint32
+U16 = mybir.dt.uint16
+U8 = mybir.dt.uint8
+E4M3X4 = mybir.dt.float8_e4m3fn_x4
+E2M1X4 = mybir.dt.float4_e2m1fn_x4
+MULT = mybir.AluOpType.mult
+COPY = mybir.ActivationFunctionType.Copy
+IDENTITY = mybir.ActivationFunctionType.Identity
+
+P = 128
+PACK = 4
+HALF = S // 2
+LIST_COLS = HALF // 16
+N_MM = 128
+FLOPS = 2 * 2 * K * M * S
+
+
+def tile_list_hboth_bias_kernel(
+    tc, xT, w4_words, w4_scales, r8_words, r8_scales, wgt, b, wgo, offs, offs2, out
+):
+    nc = tc.nc
+    with ExitStack() as ctx:
+        held = ctx.enter_context(tc.tile_pool(name="held", bufs=1))
+        psum = ctx.enter_context(tc.psum_pool(name="psum", bufs=1))
+
+        lists_in = held.tile([P, S // 16], U16, name="lists_in")
+        lists_out = held.tile([P, S // 16], U16, name="lists_out")
+        wgt_t = held.tile([P, S], F32, name="wgt_t")
+        wgo_t = held.tile([P, S], F32, name="wgo_t")
+        bias = held.tile([P, M // P], F32, name="bias")
+        planes = [held.tile([P, T], F32, name=f"plane{t}") for t in range(PACK)]
+        w4 = held.tile([P, 2 * M], U8, name="w4", align_bytes=64)
+        r8 = held.tile([P, 4 * M], U8, name="r8", align_bytes=64)
+        scales = held.tile([P, 2 * M], U8, name="scales", align_bytes=64)
+        windows = [held.tile([P, T], F32, name=f"window{m}") for m in range(M // P)]
+        picked = [held.tile([P, PACK, HALF], F32, name=f"picked{c}") for c in range(2)]
+        grouped = [held.tile([P, HALF, PACK], BF16, name=f"grouped{c}", align_bytes=64) for c in range(2)]
+        codes = [held.tile([P, HALF], U32, name=f"codes{c}", align_bytes=64) for c in range(2)]
+        xscales = [held.tile([P, HALF], U8, name=f"xscales{c}", align_bytes=64) for c in range(2)]
+        y = [[held.tile([P, HALF], F32, name=f"y{c}{m}") for m in range(M // P)] for c in range(2)]
+        acc = [
+            [[psum.tile([P, N_MM], F32, name=f"acc{c}{m}{h}") for h in range(2)] for m in range(M // P)]
+            for c in range(2)
+        ]
+
+        nc.vector.memset(scales[:].bitcast(I32), 0)
+        for m in range(M // P):
+            nc.vector.memset(windows[m][:], 0.0)
+
+        x_rows = xT.rearrange("(p j) w -> p j w", j=PACK)
+        nc.sync.dma_start(lists_in[:], offs)
+        nc.sync.dma_start(wgt_t[:], wgt)
+        nc.sync.dma_start(planes[0][:], x_rows[:, 0, :])
+        nc.sync.dma_start(planes[1][:], x_rows[:, 1, :])
+        for q in range(4):
+            nc.scalar.dma_start(
+                scales[32 * q : 32 * q + 4, 0:M].bitcast(I32),
+                w4_scales[0, 4 * q : 4 * q + 4, :].bitcast(I32),
+            )
+        for q in range(4):
+            nc.gpsimd.dma_start(
+                scales[32 * q : 32 * q + 4, M : 2 * M].bitcast(I32),
+                r8_scales[0, 4 * q : 4 * q + 4, :].bitcast(I32),
+            )
+        nc.sync.dma_start(planes[2][:], x_rows[:, 2, :])
+        nc.sync.dma_start(planes[3][:], x_rows[:, 3, :])
+        nc.sync.dma_start(r8[:].bitcast(I32), r8_words[0].rearrange("p n i -> p (n i)").bitcast(I32))
+        nc.sync.dma_start(w4[:].bitcast(I32), w4_words[0].bitcast(I32))
+        nc.sync.dma_start(lists_out[:], offs2)
+        nc.sync.dma_start(wgo_t[:], wgo)
+        with nc.allow_non_contiguous_dma(reason="one bias value to a partition"):
+            nc.gpsimd.dma_start(bias[:], b.rearrange("(m p) -> p m", p=P))
+
+        def gather(t, c):
+            nc.vector.tensor_tensor(
+                picked[c][:, t, :],
+                planes[t][:].indirect(lists_in[:, c * LIST_COLS : (c + 1) * LIST_COLS]),
+                wgt_t[:, c * HALF : (c + 1) * HALF],
+                MULT,
+            )
+
+        def group(copy, c, t0):
+            copy(
+                grouped[c][:, :, t0 : t0 + 2],
+                picked[c][:, t0 : t0 + 2, :].rearrange("p t n -> p n t"),
+            )
+
+        def quantize(c, lo, hi):
+            nc.vector.quantize_mx(
+                out=codes[c][:, lo:hi].bitcast(E4M3X4),
+                scales=xscales[c][:, lo:hi],
+                in_=grouped[c][:, lo:hi, :].rearrange("p n t -> p (n t)"),
+            )
+
+        def multiply(c, m):
+            for h in range(2):
+                cols = slice(h * N_MM, (h + 1) * N_MM)
+                nc.tensor.matmul_mx(
+                    out=acc[c][m][h][:],
+                    lhsT=w4[:, 2 * m * P : 2 * (m + 1) * P].bitcast(E2M1X4),
+                    lhsT_scale=scales[:, m * P : (m + 1) * P],
+                    rhs=codes[c][:, cols].bitcast(E4M3X4),
+                    rhs_scale=xscales[c][:, cols],
+                    start=True,
+                    stop=False,
+                )
+                nc.tensor.matmul_mx(
+                    out=acc[c][m][h][:],
+                    lhsT=r8[:, 4 * m * P : 4 * (m + 1) * P].bitcast(E4M3X4),
+                    lhsT_scale=scales[:, M + m * P : M + (m + 1) * P],
+                    rhs=codes[c][:, cols].bitcast(E4M3X4),
+                    rhs_scale=xscales[c][:, cols],
+                    start=False,
+                    stop=True,
+                )
+                nc.scalar.activation(y[c][m][:, cols], acc[c][m][h][:], IDENTITY, bias=bias[:, m : m + 1], scale=1.0)
+
+        def scatter(c, m):
+            nc.vector.tensor_tensor(
+                windows[m][:].indirect(lists_out[:, c * LIST_COLS : (c + 1) * LIST_COLS]),
+                y[c][m][:],
+                wgo_t[:, c * HALF : (c + 1) * HALF],
+                MULT,
+            )
+
+        for t in range(2):
+            gather(t, 0)
+            gather(t, 1)
+        group(nc.scalar.copy, 0, 0)
+        group(nc.scalar.copy, 1, 0)
+        gather(2, 0)
+        gather(2, 1)
+        gather(3, 0)
+        group(nc.vector.tensor_copy, 0, 2)
+        quantize(0, 0, N_MM)
+        quantize(0, N_MM, HALF)
+        multiply(0, 0)
+        gather(3, 1)
+        multiply(0, 1)
+        group(nc.scalar.copy, 1, 2)
+        quantize(1, 0, HALF)
+        multiply(1, 0)
+        multiply(1, 1)
+        for c in range(2):
+            for m in range(M // P):
+                scatter(c, m)
+                if c == 1:
+                    nc.sync.dma_start(out[m * P : (m + 1) * P, :], windows[m][:])

@@ -34,7 +34,7 @@ def tile_list_hboth_bias_kernel(
 
         lists_in = held.tile([P, S // 16], U16, name="lists_in")
         lists_out = held.tile([P, S // 16], U16, name="lists_out")
-        wgt_t = held.tile([P, S], F32, name="wgt_t")
+        wgt_t = [held.tile([P, HALF], F32, name=f"wgt_t{c}") for c in range(2)]
         wgo_t = held.tile([P, S], F32, name="wgo_t")
         bias = held.tile([P, M // P], F32, name="bias")
         planes = [held.tile([P, T], F32, name=f"plane{t}") for t in range(PACK)]
@@ -57,41 +57,45 @@ def tile_list_hboth_bias_kernel(
             nc.vector.memset(windows[m][:], 0.0)
 
         x_rows = xT.rearrange("(p j) w -> p j w", j=PACK)
+
+        def load_scales(queue, source, q, first):
+            queue.dma_start(
+                scales[32 * q : 32 * q + 4, first : first + M].bitcast(I32),
+                source[0, 4 * q : 4 * q + 4, :].bitcast(I32),
+            )
+
         nc.sync.dma_start(lists_in[:], offs)
-        nc.sync.dma_start(wgt_t[:], wgt)
+        nc.sync.dma_start(wgt_t[0][:], wgt[:, 0:HALF])
         nc.sync.dma_start(planes[0][:], x_rows[:, 0, :])
+        nc.sync.dma_start(wgt_t[1][:], wgt[:, HALF:S])
         nc.sync.dma_start(planes[1][:], x_rows[:, 1, :])
         for q in range(4):
-            nc.scalar.dma_start(
-                scales[32 * q : 32 * q + 4, 0:M].bitcast(I32),
-                w4_scales[0, 4 * q : 4 * q + 4, :].bitcast(I32),
-            )
-        for q in range(4):
-            nc.gpsimd.dma_start(
-                scales[32 * q : 32 * q + 4, M : 2 * M].bitcast(I32),
-                r8_scales[0, 4 * q : 4 * q + 4, :].bitcast(I32),
-            )
+            load_scales(nc.sync, w4_scales, q, 0)
+        for q in range(3):
+            load_scales(nc.gpsimd, r8_scales, q, M)
         nc.sync.dma_start(planes[2][:], x_rows[:, 2, :])
+        load_scales(nc.sync, r8_scales, 3, M)
         nc.sync.dma_start(planes[3][:], x_rows[:, 3, :])
         nc.sync.dma_start(r8[:].bitcast(I32), r8_words[0].rearrange("p n i -> p (n i)").bitcast(I32))
         nc.sync.dma_start(w4[:].bitcast(I32), w4_words[0].bitcast(I32))
-        nc.sync.dma_start(lists_out[:], offs2)
         nc.sync.dma_start(wgo_t[:], wgo)
+        nc.sync.dma_start(lists_out[:], offs2)
         with nc.allow_non_contiguous_dma(reason="one bias value to a partition"):
-            nc.gpsimd.dma_start(bias[:], b.rearrange("(m p) -> p m", p=P))
+            nc.sync.dma_start(bias[:], b.rearrange("(m p) -> p m", p=P))
 
-        def gather(t, c):
+        def gather(t, c, lo=0, hi=HALF):
+            first = c * HALF + lo
             nc.vector.tensor_tensor(
-                picked[c][:, t, :],
-                planes[t][:].indirect(lists_in[:, c * LIST_COLS : (c + 1) * LIST_COLS]),
-                wgt_t[:, c * HALF : (c + 1) * HALF],
+                picked[c][:, t, lo:hi],
+                planes[t][:].indirect(lists_in[:, first // 16 : (first + hi - lo) // 16]),
+                wgt_t[c][:, lo:hi],
                 MULT,
             )
 
-        def group(copy, c, t0):
+        def group(copy, c, t0, lo=0, hi=HALF):
             copy(
-                grouped[c][:, :, t0 : t0 + 2],
-                picked[c][:, t0 : t0 + 2, :].rearrange("p t n -> p n t"),
+                grouped[c][:, lo:hi, t0 : t0 + 2],
+                picked[c][:, t0 : t0 + 2, lo:hi].rearrange("p t n -> p n t"),
             )
 
         def quantize(c, lo, hi):
@@ -139,14 +143,18 @@ def tile_list_hboth_bias_kernel(
         group(nc.scalar.copy, 1, 0)
         gather(2, 0)
         gather(2, 1)
-        gather(3, 0)
-        group(nc.vector.tensor_copy, 0, 2)
-        quantize(0, 0, N_MM)
-        quantize(0, N_MM, HALF)
+        for h in range(2):
+            gather(3, 0, h * N_MM, (h + 1) * N_MM)
+        for h in range(2):
+            group(nc.scalar.copy, 0, 2, h * N_MM, (h + 1) * N_MM)
+        for h in range(2):
+            quantize(0, h * N_MM, (h + 1) * N_MM)
         multiply(0, 0)
-        gather(3, 1)
         multiply(0, 1)
-        group(nc.scalar.copy, 1, 2)
+        for h in range(2):
+            gather(3, 1, h * N_MM, (h + 1) * N_MM)
+        for h in range(2):
+            group(nc.scalar.copy, 1, 2, h * N_MM, (h + 1) * N_MM)
         quantize(1, 0, HALF)
         multiply(1, 0)
         multiply(1, 1)

from contextlib import ExitStack

import concourse.mybir as mybir

K, M, T, S = 512, 256, 1024, 512

F32 = mybir.dt.float32
BF16 = mybir.dt.bfloat16
I32 = mybir.dt.int32
U32 = mybir.dt.uint32
U16 = mybir.dt.uint16
U8 = mybir.dt.uint8
E4M3X4 = mybir.dt.float8_e4m3fn_x4
E2M1X4 = mybir.dt.float4_e2m1fn_x4
MULT = mybir.AluOpType.mult
COPY = mybir.ActivationFunctionType.Copy
IDENTITY = mybir.ActivationFunctionType.Identity

P = 128
PACK = 4
HALF = S // 2
LIST_COLS = HALF // 16
N_MM = 128
FLOPS = 2 * 2 * K * M * S


def tile_list_hboth_bias_kernel(
    tc, xT, w4_words, w4_scales, r8_words, r8_scales, wgt, b, wgo, offs, offs2, out
):
    nc = tc.nc
    with ExitStack() as ctx:
        held = ctx.enter_context(tc.tile_pool(name="held", bufs=1))
        psum = ctx.enter_context(tc.psum_pool(name="psum", bufs=1))

        lists_in = held.tile([P, S // 16], U16, name="lists_in")
        lists_out = held.tile([P, S // 16], U16, name="lists_out")
        wgt_t = [held.tile([P, HALF], F32, name=f"wgt_t{c}") for c in range(2)]
        wgo_t = held.tile([P, S], F32, name="wgo_t")
        bias = held.tile([P, M // P], F32, name="bias")
        planes = [held.tile([P, T], F32, name=f"plane{t}") for t in range(PACK)]
        w4 = held.tile([P, 2 * M], U8, name="w4", align_bytes=64)
        r8 = held.tile([P, 4 * M], U8, name="r8", align_bytes=64)
        scales = held.tile([P, 2 * M], U8, name="scales", align_bytes=64)
        windows = [held.tile([P, T], F32, name=f"window{m}") for m in range(M // P)]
        picked = [held.tile([P, PACK, HALF], F32, name=f"picked{c}") for c in range(2)]
        grouped = [held.tile([P, HALF, PACK], BF16, name=f"grouped{c}", align_bytes=64) for c in range(2)]
        codes = [held.tile([P, HALF], U32, name=f"codes{c}", align_bytes=64) for c in range(2)]
        xscales = [held.tile([P, HALF], U8, name=f"xscales{c}", align_bytes=64) for c in range(2)]
        y = [[held.tile([P, HALF], F32, name=f"y{c}{m}") for m in range(M // P)] for c in range(2)]
        acc = [
            [[psum.tile([P, N_MM], F32, name=f"acc{c}{m}{h}") for h in range(2)] for m in range(M // P)]
            for c in range(2)
        ]

        nc.vector.memset(scales[:].bitcast(I32), 0)
        for m in range(M // P):
            nc.vector.memset(windows[m][:], 0.0)

        x_rows = xT.rearrange("(p j) w -> p j w", j=PACK)

        def load_scales(queue, source, q, first):
            queue.dma_start(
                scales[32 * q : 32 * q + 4, first : first + M].bitcast(I32),
                source[0, 4 * q : 4 * q + 4, :].bitcast(I32),
            )

        nc.sync.dma_start(lists_in[:], offs)
        nc.sync.dma_start(wgt_t[0][:], wgt[:, 0:HALF])
        nc.sync.dma_start(planes[0][:], x_rows[:, 0, :])
        nc.sync.dma_start(wgt_t[1][:], wgt[:, HALF:S])
        nc.sync.dma_start(planes[1][:], x_rows[:, 1, :])
        for q in range(4):
            load_scales(nc.sync, w4_scales, q, 0)
        for q in range(3):
            load_scales(nc.gpsimd, r8_scales, q, M)
        nc.sync.dma_start(planes[2][:], x_rows[:, 2, :])
        load_scales(nc.sync, r8_scales, 3, M)
        nc.sync.dma_start(planes[3][:], x_rows[:, 3, :])
        nc.sync.dma_start(r8[:].bitcast(I32), r8_words[0].rearrange("p n i -> p (n i)").bitcast(I32))
        nc.sync.dma_start(w4[:].bitcast(I32), w4_words[0].bitcast(I32))
        nc.sync.dma_start(wgo_t[:], wgo)
        nc.sync.dma_start(lists_out[:], offs2)
        with nc.allow_non_contiguous_dma(reason="one bias value to a partition"):
            nc.sync.dma_start(bias[:], b.rearrange("(m p) -> p m", p=P))

        def gather(t, c, lo=0, hi=HALF):
            first = c * HALF + lo
            nc.vector.tensor_tensor(
                picked[c][:, t, lo:hi],
                planes[t][:].indirect(lists_in[:, first // 16 : (first + hi - lo) // 16]),
                wgt_t[c][:, lo:hi],
                MULT,
            )

        def group(copy, c, t0, lo=0, hi=HALF):
            copy(
                grouped[c][:, lo:hi, t0 : t0 + 2],
                picked[c][:, t0 : t0 + 2, lo:hi].rearrange("p t n -> p n t"),
            )

        def quantize(c, lo, hi):
            nc.vector.quantize_mx(
                out=codes[c][:, lo:hi].bitcast(E4M3X4),
                scales=xscales[c][:, lo:hi],
                in_=grouped[c][:, lo:hi, :].rearrange("p n t -> p (n t)"),
            )

        def multiply(c, m):
            for h in range(2):
                cols = slice(h * N_MM, (h + 1) * N_MM)
                nc.tensor.matmul_mx(
                    out=acc[c][m][h][:],
                    lhsT=w4[:, 2 * m * P : 2 * (m + 1) * P].bitcast(E2M1X4),
                    lhsT_scale=scales[:, m * P : (m + 1) * P],
                    rhs=codes[c][:, cols].bitcast(E4M3X4),
                    rhs_scale=xscales[c][:, cols],
                    start=True,
                    stop=False,
                )
                nc.tensor.matmul_mx(
                    out=acc[c][m][h][:],
                    lhsT=r8[:, 4 * m * P : 4 * (m + 1) * P].bitcast(E4M3X4),
                    lhsT_scale=scales[:, M + m * P : M + (m + 1) * P],
                    rhs=codes[c][:, cols].bitcast(E4M3X4),
                    rhs_scale=xscales[c][:, cols],
                    start=False,
                    stop=True,
                )
                nc.scalar.activation(y[c][m][:, cols], acc[c][m][h][:], IDENTITY, bias=bias[:, m : m + 1], scale=1.0)

        def scatter(c, m):
            nc.vector.tensor_tensor(
                windows[m][:].indirect(lists_out[:, c * LIST_COLS : (c + 1) * LIST_COLS]),
                y[c][m][:],
                wgo_t[:, c * HALF : (c + 1) * HALF],
                MULT,
            )

        for t in range(2):
            gather(t, 0)
            gather(t, 1)
        group(nc.scalar.copy, 0, 0)
        group(nc.scalar.copy, 1, 0)
        gather(2, 0)
        gather(2, 1)
        for h in range(2):
            gather(3, 0, h * N_MM, (h + 1) * N_MM)
        for h in range(2):
            group(nc.scalar.copy, 0, 2, h * N_MM, (h + 1) * N_MM)
        for h in range(2):
            quantize(0, h * N_MM, (h + 1) * N_MM)
        multiply(0, 0)
        multiply(0, 1)
        for h in range(2):
            gather(3, 1, h * N_MM, (h + 1) * N_MM)
        for h in range(2):
            group(nc.scalar.copy, 1, 2, h * N_MM, (h + 1) * N_MM)
        quantize(1, 0, HALF)
        multiply(1, 0)
        multiply(1, 1)
        for c in range(2):
            for m in range(M // P):
                scatter(c, m)
                if c == 1:
                    nc.sync.dma_start(out[m * P : (m + 1) * P, :], windows[m][:])
